import numpy as np
import ml_dtypes


def mxq(x, axis, fmt="e4m3"):
    dtype, down = {"e4m3": (ml_dtypes.float8_e4m3fn, 7), "e5m2": (ml_dtypes.float8_e5m2, 14)}[fmt]
    v = np.moveaxis(np.asarray(x, np.float32).astype(ml_dtypes.bfloat16).astype(np.float64), axis, -1)
    blocks = v.reshape(v.shape[:-1] + (-1, 32))
    amax = np.abs(blocks).max(-1, keepdims=True)
    byte = np.maximum(np.where(amax > 0, np.frexp(amax)[1] - 1 + 127, 0) - down, 1)
    scale = np.exp2(byte - 127.0)
    codes = (blocks / scale).astype(np.float32).astype(dtype).astype(np.float64)
    return np.moveaxis((codes * scale).reshape(v.shape), -1, axis)


WIDE = False


def mx_kscale(k):
    if not WIDE:
        return np.ones(k)
    levels = np.array([10, -10, 5, -5, 0])
    if k % 512:
        return np.exp2(np.random.permutation(np.resize(levels, k // 32))).repeat(32)
    a = np.empty((k // 512, 16))
    for p in range(k // 512):
        a[p, :8] = np.random.permutation(np.resize(levels, 8))
        for g in range(8):
            far = levels[np.abs(levels - a[p, g]) >= 10]
            a[p, g + 8] = far[np.random.randint(len(far))]
    return np.exp2(a.ravel()).repeat(32)


def f64(x):
    return np.asarray(x).astype(np.float64)


def striped(idx):
    return np.tile(idx.reshape(-1, 16).T, (8, 1)).astype(np.uint16)


def unstriped(offs):
    return offs[:16].T.reshape(-1).astype(np.int64)


def relu2(v):
    return np.maximum(v, 0.0) ** 2


K, T, E, C, N = 3072, 768, 2, 256, 128


def by_expert(wq, xq):
    return np.concatenate([wq[e].T @ xq[:, e * C:(e + 1) * C] for e in range(E)], axis=1)


def setup_inputs():
    n = np.random.standard_normal
    s = mx_kscale(K)[:, None]
    return {
        "xT": (n((K, T)) * s).astype(np.float32),
        "w": (n((E, K, N)) / np.sqrt(K) / s[None]).astype(np.float32),
        "b": (0.3 * n((N, E))).astype(np.float32),
        "gate": np.tile(np.random.uniform(0.2, 1.0, E * C), (N, 1)).astype(np.float32),
        "offs": striped(np.random.permutation(T)[:E * C]),
    }


def reference(xT, w, b, gate, offs):
    idx = unstriped(offs)
    xq = mxq(f64(xT)[:, idx], 0, "e4m3")
    y = by_expert(mxq(f64(w), 1, "e4m3"), xq)
    y = relu2(y + np.repeat(f64(b), C, axis=1))
    out = np.zeros((N, T))
    out[:, idx] = f64(gate) * y
    return out

@@ -1,0 +1,151 @@
+from contextlib import ExitStack
+
+import concourse.mybir as mybir
+
+K, T, E, C, N = 3072, 768, 2, 256, 128
+FLOPS = 2 * K * N * E * C
+
+F32 = mybir.dt.float32
+BF16 = mybir.dt.bfloat16
+U32 = mybir.dt.uint32
+U16 = mybir.dt.uint16
+U8 = mybir.dt.uint8
+FP8X4 = mybir.dt.float8_e4m3fn_x4
+MULT = mybir.AluOpType.mult
+RELU = mybir.ActivationFunctionType.Relu
+
+P = 128
+J = 4
+I = 4
+PASSES = K // (P * J)
+
+LAST = PASSES - 1
+X_LAST_LOADS = [(0, 512), (512, 768)]
+X_CASTS = [("gpsimd", 640, 768), ("vector", 512, 640), ("scalar", 0, 512)]
+X_LAST_CASTS = [("gpsimd", 640, 768), ("vector", 512, 640), ("vector", 448, 512), ("scalar", 0, 448)]
+X_QUANTS = [(512, 768), (0, 512)]
+W_CHUNKS = [(0, 0, 2), (0, 2, 2), (0, 4, 2), (1, 0, 2), (1, 2, 2), (1, 4, 1), (1, 5, 1)]
+BOTH = [("gpsimd", 64, 128), ("scalar", 0, 64)]
+ALONE = [("scalar", 0, 128)]
+W_LAST = [("vector", 64, 128), ("scalar", 0, 64)]
+PLANES = [(0, 0), (0, 4), (1, 0), (1, 4), (1, 8), (1, 12)]
+
+
+def tile_routed_moe_kernel(tc, xT, w, b, gate, offs, out):
+    nc = tc.nc
+    x_rows = xT.rearrange("(g p j) t -> g p j t", p=P, j=J)
+    w_rows = w.rearrange("e (g p j) n -> e p g j n", p=P, j=J)
+
+    with ExitStack() as ctx:
+        keep = ctx.enter_context(tc.tile_pool(name="keep", bufs=1))
+        pair = ctx.enter_context(tc.tile_pool(name="pair", bufs=2))
+        psum = ctx.enter_context(tc.psum_pool(name="psum", bufs=1))
+
+        offsets = keep.tile([P, E * C // 16], U16, name="offsets")
+        bias = keep.tile([P, E], F32, name="bias")
+        gates = keep.tile([P, E * C], F32, name="gates")
+
+        x_scales = [keep.tile([P, T], U8, name=f"x_scales{i}", align_bytes=64) for i in range(2)]
+        for tile in x_scales:
+            nc.gpsimd.memset(tile[:], 0)
+        window = keep.tile([P, T], F32, name="window")
+        nc.gpsimd.memset(window[:], 0.0)
+
+        w_words = [keep.tile([P, PASSES, N], U32, name=f"w_words{e}", align_bytes=64) for e in range(E)]
+        w_scales = [keep.tile([P, PASSES, N], U8, name=f"w_scales{e}", align_bytes=64) for e in range(E)]
+        sums = [psum.tile([P, C], F32, name=f"sums{e}") for e in range(E)]
+        words = []
+        picked_scales = []
+
+        def lay(engine, out, in_):
+            if engine == "gpsimd":
+                nc.gpsimd.tensor_copy(out, in_.rearrange("p j t -> p t j"))
+                return
+            out = out.rearrange("p (c i) j -> p c j i", i=I)
+            in_ = in_.rearrange("p j (c i) -> p c j i", i=I)
+            if engine == "scalar":
+                nc.scalar.copy(out, in_)
+            else:
+                nc.vector.tensor_copy(out, in_)
+
+        def gather_scales(i):
+            picked = keep.tile([P, E * C], U8, name=f"picked_scales{i}", align_bytes=64)
+            nc.vector.tensor_copy(picked[:], x_scales[i][:].indirect(offsets[:]))
+            picked_scales.append(picked)
+
+        def multiply(e, g):
+            cols = slice(e * C, (e + 1) * C)
+            i, k = PLANES[g]
+            nc.tensor.matmul_mx(
+                out=sums[e][:],
+                lhsT=w_words[e][:, g, :].bitcast(FP8X4),
+                lhsT_scale=w_scales[e][:, g, :],
+                rhs=words[g][:, cols].bitcast(FP8X4),
+                rhs_scale=picked_scales[i][k:P, cols],
+                start=(g == 0),
+                stop=(g == LAST),
+            )
+
+        for g in range(PASSES):
+            raws = []
+            for t0, t1 in X_LAST_LOADS if g == LAST else [(0, T)]:
+                raw = keep.tile([P, J, t1 - t0], F32, name=f"x_raw{g}_{t0}")
+                nc.sync.dma_start(raw[:], x_rows[g, :, :, t0:t1])
+                raws.append((t0, t1, raw))
+            if g == 0:
+                nc.sync.dma_start(offsets[:], offs)
+            laid = pair.tile([P, T, J], BF16, name="laid", align_bytes=64)
+            for r0, r1, raw in raws:
+                for engine, t0, t1 in X_LAST_CASTS if g == LAST else X_CASTS:
+                    if r0 <= t0 < r1:
+                        lay(engine, laid[:, t0:t1, :], raw[:, :, t0 - r0:t1 - r0])
+            codes = keep.tile([P, T], U32, name=f"x_words{g}", align_bytes=64)
+            i, k = PLANES[g]
+            for t0, t1 in X_QUANTS:
+                nc.vector.quantize_mx(
+                    out=codes[:, t0:t1].bitcast(FP8X4),
+                    scales=x_scales[i][k:P, t0:t1],
+                    in_=laid[:, t0:t1, :].rearrange("p t j -> p (t j)"),
+                )
+            picked = keep.tile([P, E * C], U32, name=f"picked_words{g}", align_bytes=64)
+            nc.vector.tensor_copy(picked[:], codes[:].indirect(offsets[:]))
+            words.append(picked)
+            if g == 2:
+                gather_scales(0)
+        gather_scales(1)
+        nc.sync.dma_start(bias[:], b)
+
+        def finish(e):
+            cols = slice(e * C, (e + 1) * C)
+            rectified = keep.tile([P, C], F32, name=f"rectified{e}")
+            squared = keep.tile([P, C], F32, name=f"squared{e}")
+            nc.scalar.activation(rectified[:], sums[e][:], RELU, bias=bias[:, e:e + 1])
+            nc.scalar.square(squared[:], rectified[:])
+            nc.vector.tensor_tensor(
+                window[:].indirect(offsets[:, e * C // 16:(e + 1) * C // 16]), squared[:], gates[:, cols], MULT
+            )
+
+        w_raw = {}
+        for e, g0, n in W_CHUNKS:
+            raw = keep.tile([P, n, J, N], F32, name=f"w_raw{e}_{g0}")
+            nc.sync.dma_start(raw[:], w_rows[e, :, g0:g0 + n, :, :])
+            w_raw[(e, g0)] = raw
+        nc.sync.dma_start(gates[:], gate)
+
+        for e, g0, n in W_CHUNKS:
+            raw = w_raw[(e, g0)]
+            pairs = keep.tile([P, n, N, J], BF16, name=f"w_bf{e}_{g0}", align_bytes=64)
+            for c in range(n):
+                shares = W_LAST if (e, g0) == (1, LAST) else BOTH if c == 0 else ALONE
+                for engine, n0, n1 in shares:
+                    lay(engine, pairs[:, c, n0:n1, :], raw[:, c, :, n0:n1])
+            nc.vector.quantize_mx(
+                out=w_words[e][:, g0:g0 + n, :].rearrange("p c n -> p (c n)").bitcast(FP8X4),
+                scales=w_scales[e][:, g0:g0 + n, :].rearrange("p c n -> p (c n)"),
+                in_=pairs[:].rearrange("p c n j -> p (c n j)"),
+            )
+            for g in range(g0, g0 + n):
+                multiply(e, g)
+            if g0 + n == PASSES:
+                finish(e)
+        nc.sync.dma_start(out, window[:])

@@ -12,23 +12,22 @@ U16 = mybir.dt.uint16
 U8 = mybir.dt.uint8
 FP8X4 = mybir.dt.float8_e4m3fn_x4
 MULT = mybir.AluOpType.mult
+ADD = mybir.AluOpType.add
 RELU = mybir.ActivationFunctionType.Relu
 
 P = 128
 J = 4
 I = 4
 PASSES = K // (P * J)
-
 LAST = PASSES - 1
-X_LAST_LOADS = [(0, 512), (512, 768)]
-X_CASTS = [("gpsimd", 640, 768), ("vector", 512, 640), ("scalar", 0, 512)]
-X_LAST_CASTS = [("gpsimd", 640, 768), ("vector", 512, 640), ("vector", 448, 512), ("scalar", 0, 448)]
-X_QUANTS = [(512, 768), (0, 512)]
-W_CHUNKS = [(0, 0, 2), (0, 2, 2), (0, 4, 2), (1, 0, 2), (1, 2, 2), (1, 4, 1), (1, 5, 1)]
-BOTH = [("gpsimd", 64, 128), ("scalar", 0, 64)]
-ALONE = [("scalar", 0, 128)]
-W_LAST = [("vector", 64, 128), ("scalar", 0, 64)]
 PLANES = [(0, 0), (0, 4), (1, 0), (1, 4), (1, 8), (1, 12)]
+
+X_VECTOR = [128,128,0,128,128,128]
+X_GPSIMD = [128,128,128,128,128,128]
+X_QUANTS = [(0, 512), (512, 768)]
+W_CHUNKS = [(0, 0, 2, "scalar"), (0, 2, 2, "scalar"), (0, 4, 2, "scalar"), (1, 0, 2, "gpsimd"), (1, 2, 2, "scalar"), (1, 4, 2, "vector")]
+W_GROUPS = [(0, 0, 2, "a"), (0, 2, 2, "b"), (0, 4, 2, "c"), (1, 0, 4, "d"), (1, 4, 2, "d")]
+W_STEPS = [("cast", 0), ("quantise", 0), ("multiply", 0), ("scales", "a"), ("cast", 1), ("quantise", 1), ("multiply", 1), ("cast", 2), ("quantise", 2), ("multiply", 2), ("cast", 3), ("cast", 4), ("quantise", 3), ("multiply", 3), ("cast", 5), ("quantise", 4), ("multiply", 4)]
 
 
 def tile_routed_moe_kernel(tc, xT, w, b, gate, offs, out):
@@ -57,19 +56,22 @@ def tile_routed_moe_kernel(tc, xT, w, b, gate, offs, out):
         words = []
         picked_scales = []
 
-        def lay(engine, out, in_):
-            if engine == "gpsimd":
-                nc.gpsimd.tensor_copy(out, in_.rearrange("p j t -> p t j"))
-                return
-            out = out.rearrange("p (c i) j -> p c j i", i=I)
-            in_ = in_.rearrange("p j (c i) -> p c j i", i=I)
+        def copy_on(engine, out, in_):
             if engine == "scalar":
                 nc.scalar.copy(out, in_)
+            elif engine == "gpsimd":
+                nc.gpsimd.tensor_copy(out, in_)
             else:
                 nc.vector.tensor_copy(out, in_)
 
-        def gather_scales(i):
-            picked = keep.tile([P, E * C], U8, name=f"picked_scales{i}", align_bytes=64)
+        def lay(engine, out, in_):
+            if engine == "gpsimd":
+                copy_on(engine, out, in_.rearrange("p j t -> p t j"))
+                return
+            copy_on(engine, out.rearrange("p (c i) j -> p c j i", i=I), in_.rearrange("p j (c i) -> p c j i", i=I))
+
+        def gather_scales(i, tag):
+            picked = keep.tile([P, E * C], U8, name=f"picked_scales{i}", tag=tag, align_bytes=64)
             nc.vector.tensor_copy(picked[:], x_scales[i][:].indirect(offsets[:]))
             picked_scales.append(picked)
 
@@ -87,18 +89,18 @@ def tile_routed_moe_kernel(tc, xT, w, b, gate, offs, out):
             )
 
         for g in range(PASSES):
-            raws = []
-            for t0, t1 in X_LAST_LOADS if g == LAST else [(0, T)]:
-                raw = keep.tile([P, J, t1 - t0], F32, name=f"x_raw{g}_{t0}")
-                nc.sync.dma_start(raw[:], x_rows[g, :, :, t0:t1])
-                raws.append((t0, t1, raw))
+            raw = keep.tile([P, J, T], F32, name=f"x_raw{g}")
+            nc.sync.dma_start(raw[:], x_rows[g])
             if g == 0:
                 nc.sync.dma_start(offsets[:], offs)
+            if g == 1:
+                nc.sync.dma_start(bias[:], b)
             laid = pair.tile([P, T, J], BF16, name="laid", align_bytes=64)
-            for r0, r1, raw in raws:
-                for engine, t0, t1 in X_LAST_CASTS if g == LAST else X_CASTS:
-                    if r0 <= t0 < r1:
-                        lay(engine, laid[:, t0:t1, :], raw[:, :, t0 - r0:t1 - r0])
+            v = X_VECTOR[g]
+            s = T - X_GPSIMD[g]
+            for engine, t0, t1 in [("gpsimd", s, T), ("vector", 0, v), ("scalar", v, 512), ("scalar", 512, s)]:
+                if t1 > t0:
+                    lay(engine, laid[:, t0:t1, :], raw[:, :, t0:t1])
             codes = keep.tile([P, T], U32, name=f"x_words{g}", align_bytes=64)
             i, k = PLANES[g]
             for t0, t1 in X_QUANTS:
@@ -110,42 +112,57 @@ def tile_routed_moe_kernel(tc, xT, w, b, gate, offs, out):
             picked = keep.tile([P, E * C], U32, name=f"picked_words{g}", align_bytes=64)
             nc.vector.tensor_copy(picked[:], codes[:].indirect(offsets[:]))
             words.append(picked)
-            if g == 2:
-                gather_scales(0)
-        gather_scales(1)
-        nc.sync.dma_start(bias[:], b)
+            if g == 1:
+                gather_scales(0, "picked0")
 
-        def finish(e):
+        w_raw = []
+        for e, g0, n, engine in W_CHUNKS:
+            raw = keep.tile([P, n, J, N], F32, name=f"w_raw{e}_{g0}", tag=f"w_raw{e}_{g0}")
+            nc.sync.dma_start(raw[:], w_rows[e, :, g0:g0 + n, :, :])
+            w_raw.append(raw)
+        nc.sync.dma_start(gates[:], gate)
+
+        w_laid = {}
+        for step in W_STEPS:
+            if step[0] == "scales":
+                gather_scales(1, step[1])
+            elif step[0] == "cast":
+                e, g0, n, engine = W_CHUNKS[step[1]]
+                q0, qn, tag = [group[1:] for group in W_GROUPS if group[0] == e and group[1] <= g0 < group[1] + group[2]][0]
+                if (e, q0) not in w_laid:
+                    w_laid[(e, q0)] = keep.tile([P, qn, N, J], BF16, name=f"w_laid{e}_{q0}", tag=tag, align_bytes=64)
+                laid_w = w_laid[(e, q0)][:, g0 - q0:g0 - q0 + n, :, :]
+                raw_w = w_raw[step[1]]
+                if engine == "gpsimd":
+                    for c in range(n):
+                        nc.gpsimd.tensor_scalar(
+                            laid_w[:, c, :, :], raw_w[:, c, :, :].rearrange("p j t -> p t j"), 1.0, 0.0, MULT, ADD
+                        )
+                else:
+                    copy_on(
+                        engine,
+                        laid_w.rearrange("p g (c i) j -> p g c j i", i=I),
+                        raw_w[:].rearrange("p g j (c i) -> p g c j i", i=I),
+                    )
+            elif step[0] == "quantise":
+                e, g0, n, tag = W_GROUPS[step[1]]
+                nc.vector.quantize_mx(
+                    out=w_words[e][:, g0:g0 + n, :].rearrange("p c n -> p (c n)").bitcast(FP8X4),
+                    scales=w_scales[e][:, g0:g0 + n, :].rearrange("p c n -> p (c n)"),
+                    in_=w_laid[(e, g0)][:].rearrange("p c n j -> p (c n j)"),
+                )
+            else:
+                e, g0, n, tag = W_GROUPS[step[1]]
+                for g in range(g0, g0 + n):
+                    multiply(e, g)
+
+        for e in range(E):
             cols = slice(e * C, (e + 1) * C)
-            rectified = keep.tile([P, C], F32, name=f"rectified{e}")
-            squared = keep.tile([P, C], F32, name=f"squared{e}")
+            rectified = keep.tile([P, C], F32, name=f"rectified{e}", tag=("w_raw1_2", "w_raw1_2")[e])
+            squared = keep.tile([P, C], F32, name=f"squared{e}", tag=("w_raw1_4", "squared")[e])
             nc.scalar.activation(rectified[:], sums[e][:], RELU, bias=bias[:, e:e + 1])
             nc.scalar.square(squared[:], rectified[:])
             nc.vector.tensor_tensor(
                 window[:].indirect(offsets[:, e * C // 16:(e + 1) * C // 16]), squared[:], gates[:, cols], MULT
             )
-
-        w_raw = {}
-        for e, g0, n in W_CHUNKS:
-            raw = keep.tile([P, n, J, N], F32, name=f"w_raw{e}_{g0}")
-            nc.sync.dma_start(raw[:], w_rows[e, :, g0:g0 + n, :, :])
-            w_raw[(e, g0)] = raw
-        nc.sync.dma_start(gates[:], gate)
-
-        for e, g0, n in W_CHUNKS:
-            raw = w_raw[(e, g0)]
-            pairs = keep.tile([P, n, N, J], BF16, name=f"w_bf{e}_{g0}", align_bytes=64)
-            for c in range(n):
-                shares = W_LAST if (e, g0) == (1, LAST) else BOTH if c == 0 else ALONE
-                for engine, n0, n1 in shares:
-                    lay(engine, pairs[:, c, n0:n1, :], raw[:, c, :, n0:n1])
-            nc.vector.quantize_mx(
-                out=w_words[e][:, g0:g0 + n, :].rearrange("p c n -> p (c n)").bitcast(FP8X4),
-                scales=w_scales[e][:, g0:g0 + n, :].rearrange("p c n -> p (c n)"),
-                in_=pairs[:].rearrange("p c n j -> p (c n j)"),
-            )
-            for g in range(g0, g0 + n):
-                multiply(e, g)
-            if g0 + n == PASSES:
-                finish(e)
         nc.sync.dma_start(out, window[:])

@@ -12,7 +12,6 @@ U16 = mybir.dt.uint16
 U8 = mybir.dt.uint8
 FP8X4 = mybir.dt.float8_e4m3fn_x4
 MULT = mybir.AluOpType.mult
-ADD = mybir.AluOpType.add
 RELU = mybir.ActivationFunctionType.Relu
 
 P = 128
@@ -21,13 +20,13 @@ I = 4
 PASSES = K // (P * J)
 LAST = PASSES - 1
 PLANES = [(0, 0), (0, 4), (1, 0), (1, 4), (1, 8), (1, 12)]
+ADD = mybir.AluOpType.add
 
 X_VECTOR = [128,128,0,128,128,128]
 X_GPSIMD = [128,128,128,128,128,128]
+X_PIECES = [5]
 X_QUANTS = [(0, 512), (512, 768)]
-W_CHUNKS = [(0, 0, 2, "scalar"), (0, 2, 2, "scalar"), (0, 4, 2, "scalar"), (1, 0, 2, "gpsimd"), (1, 2, 2, "scalar"), (1, 4, 2, "vector")]
-W_GROUPS = [(0, 0, 2, "a"), (0, 2, 2, "b"), (0, 4, 2, "c"), (1, 0, 4, "d"), (1, 4, 2, "d")]
-W_STEPS = [("cast", 0), ("quantise", 0), ("multiply", 0), ("scales", "a"), ("cast", 1), ("quantise", 1), ("multiply", 1), ("cast", 2), ("quantise", 2), ("multiply", 2), ("cast", 3), ("cast", 4), ("quantise", 3), ("multiply", 3), ("cast", 5), ("quantise", 4), ("multiply", 4)]
+W_LOADS = [(0, 0, 2), (0, 2, 2), (0, 4, 2), (1, 0, 2), (1, 2, 1), (1, 3, 1), (1, 4, 1), (1, 5, 1)]
 
 
 def tile_routed_moe_kernel(tc, xT, w, b, gate, offs, out):
@@ -37,132 +36,177 @@ def tile_routed_moe_kernel(tc, xT, w, b, gate, offs, out):
 
     with ExitStack() as ctx:
         keep = ctx.enter_context(tc.tile_pool(name="keep", bufs=1))
-        pair = ctx.enter_context(tc.tile_pool(name="pair", bufs=2))
         psum = ctx.enter_context(tc.psum_pool(name="psum", bufs=1))
 
-        offsets = keep.tile([P, E * C // 16], U16, name="offsets")
-        bias = keep.tile([P, E], F32, name="bias")
-        gates = keep.tile([P, E * C], F32, name="gates")
+        def tile(shape, dtype, name, buffer=None):
+            return keep.tile(shape, dtype, name=name, tag=buffer or name, align_bytes=64)
 
-        x_scales = [keep.tile([P, T], U8, name=f"x_scales{i}", align_bytes=64) for i in range(2)]
-        for tile in x_scales:
-            nc.gpsimd.memset(tile[:], 0)
-        window = keep.tile([P, T], F32, name="window")
+        offsets = keep.tile([P, E * C // 16], U16, name="offsets")
+        bias = tile([P, E], F32, "bias")
+        gates = tile([P, E * C], F32, "gates")
+
+        x_scales = [tile([P, T], U8, f"x_scales{i}") for i in range(2)]
+        for plane in x_scales:
+            nc.gpsimd.memset(plane[:], 0)
+        window = tile([P, T], F32, "window")
         nc.gpsimd.memset(window[:], 0.0)
 
-        w_words = [keep.tile([P, PASSES, N], U32, name=f"w_words{e}", align_bytes=64) for e in range(E)]
-        w_scales = [keep.tile([P, PASSES, N], U8, name=f"w_scales{e}", align_bytes=64) for e in range(E)]
         sums = [psum.tile([P, C], F32, name=f"sums{e}") for e in range(E)]
-        words = []
-        picked_scales = []
+        x_words = []
+        gathered = {}
+        w_raw = {}
+        w_laid = {}
+        w_codes = {}
 
-        def copy_on(engine, out, in_):
+        def listed(e0, e1):
+            return offsets[:, e0 * C // 16:e1 * C // 16]
+
+        def lay(engine, out, in_):
+            out = out.rearrange("p g (c i) j -> p g c j i", i=I)
+            in_ = in_.rearrange("p g j (c i) -> p g c j i", i=I)
             if engine == "scalar":
                 nc.scalar.copy(out, in_)
-            elif engine == "gpsimd":
-                nc.gpsimd.tensor_copy(out, in_)
             else:
                 nc.vector.tensor_copy(out, in_)
 
-        def lay(engine, out, in_):
+        def gather(window_tile, dtype, name, key, e0, e1, buffer=None):
+            picked = tile([P, (e1 - e0) * C], dtype, f"{name}_{e0}", buffer)
+            nc.vector.tensor_copy(picked[:], window_tile[:].indirect(listed(e0, e1)))
+            for e in range(e0, e1):
+                gathered[(key, e)] = (picked, (e - e0) * C)
+
+        def gather_words(g, e0, e1, buffer=None):
+            gather(x_words[g], U32, f"picked_words{g}", ("words", g), e0, e1, buffer)
+
+        def gather_scales(i, e0, e1, buffer=None):
+            gather(x_scales[i], U8, f"picked_scales{i}", ("scales", i), e0, e1, buffer)
+
+        def group(e, g0, n, buffer=None):
+            laid = tile([P, n, N, J], BF16, f"w_laid{e}_{g0}", buffer)
+            for c in range(n):
+                w_laid[(e, g0 + c)] = (laid, c)
+
+        def cast(engine, e, g0, n):
+            raw, r = w_raw[(e, g0)]
+            laid, c = w_laid[(e, g0)]
             if engine == "gpsimd":
-                copy_on(engine, out, in_.rearrange("p j t -> p t j"))
-                return
-            copy_on(engine, out.rearrange("p (c i) j -> p c j i", i=I), in_.rearrange("p j (c i) -> p c j i", i=I))
+                for d in range(n):
+                    nc.gpsimd.tensor_scalar(
+                        laid[:, c + d, :, :], raw[:, r + d, :, :].rearrange("p j t -> p t j"), 1.0, 0.0, MULT, ADD
+                    )
+            else:
+                lay(engine, laid[:, c:c + n, :, :], raw[:, r:r + n, :, :])
 
-        def gather_scales(i, tag):
-            picked = keep.tile([P, E * C], U8, name=f"picked_scales{i}", tag=tag, align_bytes=64)
-            nc.vector.tensor_copy(picked[:], x_scales[i][:].indirect(offsets[:]))
-            picked_scales.append(picked)
+        def quantise(e, g0, n):
+            laid, c = w_laid[(e, g0)]
+            codes = tile([P, n, N], U32, f"w_words{e}_{g0}")
+            scales = tile([P, n, N], U8, f"w_scales{e}_{g0}")
+            nc.vector.quantize_mx(
+                out=codes[:].rearrange("p c n -> p (c n)").bitcast(FP8X4),
+                scales=scales[:].rearrange("p c n -> p (c n)"),
+                in_=laid[:, c:c + n, :, :].rearrange("p c n j -> p (c n j)"),
+            )
+            for d in range(n):
+                w_codes[(e, g0 + d)] = (codes[:, d, :], scales[:, d, :])
 
-        def multiply(e, g):
-            cols = slice(e * C, (e + 1) * C)
-            i, k = PLANES[g]
-            nc.tensor.matmul_mx(
-                out=sums[e][:],
-                lhsT=w_words[e][:, g, :].bitcast(FP8X4),
-                lhsT_scale=w_scales[e][:, g, :],
-                rhs=words[g][:, cols].bitcast(FP8X4),
-                rhs_scale=picked_scales[i][k:P, cols],
-                start=(g == 0),
-                stop=(g == LAST),
+        def multiply(e, g0, n):
+            for g in range(g0, g0 + n):
+                i, k = PLANES[g]
+                words, c0 = gathered[(("words", g), e)]
+                scales, c1 = gathered[(("scales", i), e)]
+                nc.tensor.matmul_mx(
+                    out=sums[e][:],
+                    lhsT=w_codes[(e, g)][0].bitcast(FP8X4),
+                    lhsT_scale=w_codes[(e, g)][1],
+                    rhs=words[:, c0:c0 + C].bitcast(FP8X4),
+                    rhs_scale=scales[k:P, c1:c1 + C],
+                    start=(g == 0),
+                    stop=(g == LAST),
+                )
+
+        rectified = {}
+
+        def rectify(e, buffer=None):
+            rectified[e] = tile([P, C], F32, f"rectified{e}", buffer)
+            nc.scalar.activation(rectified[e][:], sums[e][:], RELU, bias=bias[:, e:e + 1])
+
+        def finish(e, buffer=None):
+            squared = tile([P, C], F32, f"squared{e}", buffer)
+            nc.scalar.square(squared[:], rectified[e][:])
+            nc.vector.tensor_tensor(
+                window[:].indirect(listed(e, e + 1)), squared[:], gates[:, e * C:(e + 1) * C], MULT
             )
 
+        def load(e, g0, n):
+            raw = tile([P, n, J, N], F32, f"w_raw{e}_{g0}")
+            nc.sync.dma_start(raw[:], w_rows[e, :, g0:g0 + n, :, :])
+            for c in range(n):
+                w_raw[(e, g0 + c)] = (raw, c)
+
         for g in range(PASSES):
-            raw = keep.tile([P, J, T], F32, name=f"x_raw{g}")
-            nc.sync.dma_start(raw[:], x_rows[g])
+            pieces = []
+            for r0, r1 in X_QUANTS if g in X_PIECES else [(0, T)]:
+                raw = tile([P, 1, J, r1 - r0], F32, f"x_raw{g}_{r0}")
+                nc.sync.dma_start(raw[:, 0, :, :], x_rows[g, :, :, r0:r1])
+                pieces.append((r0, raw))
             if g == 0:
                 nc.sync.dma_start(offsets[:], offs)
             if g == 1:
                 nc.sync.dma_start(bias[:], b)
-            laid = pair.tile([P, T, J], BF16, name="laid", align_bytes=64)
+            laid = tile([P, 1, T, J], BF16, f"laid{g}", f"laid{g % 2}")
             v = X_VECTOR[g]
             s = T - X_GPSIMD[g]
-            for engine, t0, t1 in [("gpsimd", s, T), ("vector", 0, v), ("scalar", v, 512), ("scalar", 512, s)]:
+            if s < T:
+                r0, raw = pieces[-1]
+                nc.gpsimd.tensor_copy(laid[:, 0, s:T, :], raw[:, 0, :, s - r0:T - r0].rearrange("p j t -> p t j"))
+            for engine, t0, t1 in [("vector", 0, v), ("scalar", v, 512), ("scalar", 512, s)]:
                 if t1 > t0:
-                    lay(engine, laid[:, t0:t1, :], raw[:, :, t0:t1])
-            codes = keep.tile([P, T], U32, name=f"x_words{g}", align_bytes=64)
+                    r0, raw = [piece for piece in pieces if piece[0] <= t0][-1]
+                    lay(engine, laid[:, :, t0:t1, :], raw[:, :, :, t0 - r0:t1 - r0])
+            codes = tile([P, T], U32, f"x_words{g}")
             i, k = PLANES[g]
             for t0, t1 in X_QUANTS:
                 nc.vector.quantize_mx(
                     out=codes[:, t0:t1].bitcast(FP8X4),
                     scales=x_scales[i][k:P, t0:t1],
-                    in_=laid[:, t0:t1, :].rearrange("p t j -> p (t j)"),
+                    in_=laid[:, 0, t0:t1, :].rearrange("p t j -> p (t j)"),
                 )
-            picked = keep.tile([P, E * C], U32, name=f"picked_words{g}", align_bytes=64)
-            nc.vector.tensor_copy(picked[:], codes[:].indirect(offsets[:]))
-            words.append(picked)
+            x_words.append(codes)
+            if g < LAST:
+                gather_words(g, 0, E)
             if g == 1:
-                gather_scales(0, "picked0")
+                gather_scales(0, 0, E)
 
-        w_raw = []
-        for e, g0, n, engine in W_CHUNKS:
-            raw = keep.tile([P, n, J, N], F32, name=f"w_raw{e}_{g0}", tag=f"w_raw{e}_{g0}")
-            nc.sync.dma_start(raw[:], w_rows[e, :, g0:g0 + n, :, :])
-            w_raw.append(raw)
+        for chunk in W_LOADS:
+            load(*chunk)
         nc.sync.dma_start(gates[:], gate)
 
-        w_laid = {}
-        for step in W_STEPS:
-            if step[0] == "scales":
-                gather_scales(1, step[1])
-            elif step[0] == "cast":
-                e, g0, n, engine = W_CHUNKS[step[1]]
-                q0, qn, tag = [group[1:] for group in W_GROUPS if group[0] == e and group[1] <= g0 < group[1] + group[2]][0]
-                if (e, q0) not in w_laid:
-                    w_laid[(e, q0)] = keep.tile([P, qn, N, J], BF16, name=f"w_laid{e}_{q0}", tag=tag, align_bytes=64)
-                laid_w = w_laid[(e, q0)][:, g0 - q0:g0 - q0 + n, :, :]
-                raw_w = w_raw[step[1]]
-                if engine == "gpsimd":
-                    for c in range(n):
-                        nc.gpsimd.tensor_scalar(
-                            laid_w[:, c, :, :], raw_w[:, c, :, :].rearrange("p j t -> p t j"), 1.0, 0.0, MULT, ADD
-                        )
-                else:
-                    copy_on(
-                        engine,
-                        laid_w.rearrange("p g (c i) j -> p g c j i", i=I),
-                        raw_w[:].rearrange("p g j (c i) -> p g c j i", i=I),
-                    )
-            elif step[0] == "quantise":
-                e, g0, n, tag = W_GROUPS[step[1]]
-                nc.vector.quantize_mx(
-                    out=w_words[e][:, g0:g0 + n, :].rearrange("p c n -> p (c n)").bitcast(FP8X4),
-                    scales=w_scales[e][:, g0:g0 + n, :].rearrange("p c n -> p (c n)"),
-                    in_=w_laid[(e, g0)][:].rearrange("p c n j -> p (c n j)"),
-                )
-            else:
-                e, g0, n, tag = W_GROUPS[step[1]]
-                for g in range(g0, g0 + n):
-                    multiply(e, g)
-
-        for e in range(E):
-            cols = slice(e * C, (e + 1) * C)
-            rectified = keep.tile([P, C], F32, name=f"rectified{e}", tag=("w_raw1_2", "w_raw1_2")[e])
-            squared = keep.tile([P, C], F32, name=f"squared{e}", tag=("w_raw1_4", "squared")[e])
-            nc.scalar.activation(rectified[:], sums[e][:], RELU, bias=bias[:, e:e + 1])
-            nc.scalar.square(squared[:], rectified[:])
-            nc.vector.tensor_tensor(
-                window[:].indirect(offsets[:, e * C // 16:(e + 1) * C // 16]), squared[:], gates[:, cols], MULT
-            )
+        gather_words(LAST, 0, 1)
+        gather_scales(1, 0, 1)
+        group(0, 0, 4)
+        cast("scalar", 0, 0, 2)
+        cast("scalar", 0, 2, 2)
+        quantise(0, 0, 4)
+        multiply(0, 0, 4)
+        gather_words(LAST, 1, 2, "w_laid0_0")
+        group(0, 4, 2)
+        cast("scalar", 0, 4, 2)
+        quantise(0, 4, 2)
+        multiply(0, 4, 2)
+        gather_scales(1, 1, 2, "w_laid0_4")
+        group(1, 0, 4)
+        cast("scalar", 1, 0, 2)
+        cast("gpsimd", 1, 2, 1)
+        cast("scalar", 1, 3, 1)
+        rectify(0, "w_raw1_3")
+        quantise(1, 0, 4)
+        multiply(1, 0, 4)
+        group(1, 4, 2, "w_raw1_2")
+        cast("scalar", 1, 4, 1)
+        cast("vector", 1, 5, 1)
+        quantise(1, 4, 2)
+        multiply(1, 4, 2)
+        finish(0, "w_raw1_5")
+        rectify(1)
+        finish(1)
         nc.sync.dma_start(out, window[:])

@@ -16,7 +16,7 @@ RELU = mybir.ActivationFunctionType.Relu
 
 P = 128
 J = 4
-I = 4
+I = 2
 PASSES = K // (P * J)
 LAST = PASSES - 1
 PLANES = [(0, 0), (0, 4), (1, 0), (1, 4), (1, 8), (1, 12)]

@@ -146,8 +146,8 @@ def tile_routed_moe_kernel(tc, xT, w, b, gate, offs, out):
         for g in range(PASSES):
             pieces = []
             for r0, r1 in X_QUANTS if g in X_PIECES else [(0, T)]:
-                raw = tile([P, 1, J, r1 - r0], F32, f"x_raw{g}_{r0}")
-                nc.sync.dma_start(raw[:, 0, :, :], x_rows[g, :, :, r0:r1])
+                raw = tile([P, 1, J, r1 - r0 + 16], F32, f"x_raw{g}_{r0}")
+                nc.sync.dma_start(raw[:, 0, :, 0:r1 - r0], x_rows[g, :, :, r0:r1])
                 pieces.append((r0, raw))
             if g == 0:
                 nc.sync.dma_start(offsets[:], offs)

@@ -12,27 +12,26 @@ U16 = mybir.dt.uint16
 U8 = mybir.dt.uint8
 FP8X4 = mybir.dt.float8_e4m3fn_x4
 MULT = mybir.AluOpType.mult
+ADD = mybir.AluOpType.add
 RELU = mybir.ActivationFunctionType.Relu
 
 P = 128
-J = 4
-I = 2
-PASSES = K // (P * J)
+PACK = 4
+PAIR = 2
+PASSES = K // (P * PACK)
 LAST = PASSES - 1
 PLANES = [(0, 0), (0, 4), (1, 0), (1, 4), (1, 8), (1, 12)]
-ADD = mybir.AluOpType.add
-
-X_VECTOR = [128,128,0,128,128,128]
-X_GPSIMD = [128,128,128,128,128,128]
-X_PIECES = [5]
-X_QUANTS = [(0, 512), (512, 768)]
+LONG = 512
+EARLY_VECTOR = [384, 320]
+LAST_VECTOR = 128
+GPSIMD_TOKENS = 128
 W_LOADS = [(0, 0, 2), (0, 2, 2), (0, 4, 2), (1, 0, 2), (1, 2, 1), (1, 3, 1), (1, 4, 1), (1, 5, 1)]
 
 
 def tile_routed_moe_kernel(tc, xT, w, b, gate, offs, out):
     nc = tc.nc
-    x_rows = xT.rearrange("(g p j) t -> g p j t", p=P, j=J)
-    w_rows = w.rearrange("e (g p j) n -> e p g j n", p=P, j=J)
+    x_rows = xT.rearrange("(g p j) t -> g p j t", p=P, j=PACK)
+    w_rows = w.rearrange("e (g p j) n -> e p g j n", p=P, j=PACK)
 
     with ExitStack() as ctx:
         keep = ctx.enter_context(tc.tile_pool(name="keep", bufs=1))
@@ -44,45 +43,96 @@ def tile_routed_moe_kernel(tc, xT, w, b, gate, offs, out):
         offsets = keep.tile([P, E * C // 16], U16, name="offsets")
         bias = tile([P, E], F32, "bias")
         gates = tile([P, E * C], F32, "gates")
-
         x_scales = [tile([P, T], U8, f"x_scales{i}") for i in range(2)]
         for plane in x_scales:
             nc.gpsimd.memset(plane[:], 0)
         window = tile([P, T], F32, "window")
         nc.gpsimd.memset(window[:], 0.0)
-
         sums = [psum.tile([P, C], F32, name=f"sums{e}") for e in range(E)]
-        x_words = []
-        gathered = {}
-        w_raw = {}
-        w_laid = {}
-        w_codes = {}
 
-        def listed(e0, e1):
+        def slots(e0, e1):
             return offsets[:, e0 * C // 16:e1 * C // 16]
 
-        def lay(engine, out, in_):
-            out = out.rearrange("p g (c i) j -> p g c j i", i=I)
-            in_ = in_.rearrange("p g j (c i) -> p g c j i", i=I)
+        def interleave(engine, laid, raw):
+            if engine == "gpsimd":
+                nc.gpsimd.tensor_copy(laid[:, 0, :, :], raw[:, 0, :, :].rearrange("p j t -> p t j"))
+                return
+            laid = laid.rearrange("p g (c i) j -> p g c j i", i=PAIR)
+            raw = raw.rearrange("p g j (c i) -> p g c j i", i=PAIR)
             if engine == "scalar":
-                nc.scalar.copy(out, in_)
+                nc.scalar.copy(laid, raw)
             else:
-                nc.vector.tensor_copy(out, in_)
+                nc.vector.tensor_copy(laid, raw)
 
-        def gather(window_tile, dtype, name, key, e0, e1, buffer=None):
-            picked = tile([P, (e1 - e0) * C], dtype, f"{name}_{e0}", buffer)
-            nc.vector.tensor_copy(picked[:], window_tile[:].indirect(listed(e0, e1)))
+        x_words = []
+        picked = {}
+
+        def gather(sort, index, e0, e1, buffer=None):
+            source, dtype = (x_words[index], U32) if sort == "words" else (x_scales[index], U8)
+            dense = tile([P, (e1 - e0) * C], dtype, f"picked_{sort}{index}_{e0}", buffer)
+            nc.vector.tensor_copy(dense[:], source[:].indirect(slots(e0, e1)))
             for e in range(e0, e1):
-                gathered[(key, e)] = (picked, (e - e0) * C)
+                picked[(sort, index, e)] = (dense, (e - e0) * C)
 
-        def gather_words(g, e0, e1, buffer=None):
-            gather(x_words[g], U32, f"picked_words{g}", ("words", g), e0, e1, buffer)
+        for g in range(PASSES):
+            if g < LAST:
+                raw = tile([P, 1, PACK, T], F32, f"x_raw{g}")
+                nc.sync.dma_start(raw[:, 0, :, :], x_rows[g])
+                raw_long, raw_short = raw[:, :, :, 0:LONG], raw[:, :, :, LONG:T]
+            else:
+                first = tile([P, 1, PACK, LONG], F32, "x_raw_long")
+                nc.sync.dma_start(first[:, 0, :, :], x_rows[g, :, :, 0:LONG])
+                second = tile([P, 1, PACK, T - LONG], F32, "x_raw_short")
+                nc.sync.dma_start(second[:, 0, :, :], x_rows[g, :, :, LONG:T])
+                raw_long, raw_short = first[:], second[:]
+            if g == 0:
+                nc.sync.dma_start(offsets[:], offs)
+            laid_long = tile([P, 1, LONG, PACK], BF16, f"laid_long{g}", f"laid_long{g % 2}")
+            laid_short = tile([P, 1, T - LONG, PACK], BF16, f"laid_short{g}", "laid_short")
+            parts = [(0, LONG, laid_long), (LONG, T, laid_short)]
+            if g < len(EARLY_VECTOR):
+                v = EARLY_VECTOR[g]
+                interleave("vector", laid_long[:, :, 0:v, :], raw_long[:, :, :, 0:v])
+                interleave("scalar", laid_short[:], raw_short)
+                interleave("scalar", laid_long[:, :, v:LONG, :], raw_long[:, :, :, v:LONG])
+                parts = parts[::-1]
+            else:
+                v = LAST_VECTOR if g == LAST else 0
+                if v:
+                    interleave("vector", laid_long[:, :, 0:v, :], raw_long[:, :, :, 0:v])
+                    gather("words", g - 1, 0, E)
+                s = T - LONG - GPSIMD_TOKENS
+                interleave("gpsimd", laid_short[:, :, s:T - LONG, :], raw_short[:, :, :, s:T - LONG])
+                interleave("scalar", laid_long[:, :, v:LONG, :], raw_long[:, :, :, v:LONG])
+                interleave("scalar", laid_short[:, :, 0:s, :], raw_short[:, :, :, 0:s])
+            words = tile([P, T], U32, f"x_words{g}")
+            i, k = PLANES[g]
+            for t0, t1, laid in parts:
+                nc.vector.quantize_mx(
+                    out=words[:, t0:t1].bitcast(FP8X4),
+                    scales=x_scales[i][k:P, t0:t1],
+                    in_=laid[:].rearrange("p g t j -> p (g t j)"),
+                )
+            x_words.append(words)
+            if g < LAST - 1:
+                gather("words", g, 0, E)
+            if g == 1:
+                gather("scales", 0, 0, E)
 
-        def gather_scales(i, e0, e1, buffer=None):
-            gather(x_scales[i], U8, f"picked_scales{i}", ("scales", i), e0, e1, buffer)
+        w_raw = {}
+        for e, g0, n in W_LOADS:
+            raw = tile([P, n, PACK, N], F32, f"w_raw{e}_{g0}")
+            nc.sync.dma_start(raw[:], w_rows[e, :, g0:g0 + n, :, :])
+            for c in range(n):
+                w_raw[(e, g0 + c)] = (raw, c)
+            if (e, g0) == (1, 3):
+                nc.sync.dma_start(bias[:], b)
+        nc.sync.dma_start(gates[:], gate)
+
+        w_laid = {}
 
         def group(e, g0, n, buffer=None):
-            laid = tile([P, n, N, J], BF16, f"w_laid{e}_{g0}", buffer)
+            laid = tile([P, n, N, PACK], BF16, f"w_laid{e}_{g0}", buffer)
             for c in range(n):
                 w_laid[(e, g0 + c)] = (laid, c)
 
@@ -90,16 +140,15 @@ def tile_routed_moe_kernel(tc, xT, w, b, gate, offs, out):
             raw, r = w_raw[(e, g0)]
             laid, c = w_laid[(e, g0)]
             if engine == "gpsimd":
-                for d in range(n):
-                    nc.gpsimd.tensor_scalar(
-                        laid[:, c + d, :, :], raw[:, r + d, :, :].rearrange("p j t -> p t j"), 1.0, 0.0, MULT, ADD
-                    )
+                nc.gpsimd.tensor_scalar(
+                    laid[:, c, :, :], raw[:, r, :, :].rearrange("p j t -> p t j"), 1.0, 0.0, MULT, ADD
+                )
             else:
-                lay(engine, laid[:, c:c + n, :, :], raw[:, r:r + n, :, :])
+                interleave(engine, laid[:, c:c + n, :, :], raw[:, r:r + n, :, :])
 
-        def quantise(e, g0, n):
+        def multiply(e, g0, n, buffer=None):
             laid, c = w_laid[(e, g0)]
-            codes = tile([P, n, N], U32, f"w_words{e}_{g0}")
+            codes = tile([P, n, N], U32, f"w_words{e}_{g0}", buffer)
             scales = tile([P, n, N], U8, f"w_scales{e}_{g0}")
             nc.vector.quantize_mx(
                 out=codes[:].rearrange("p c n -> p (c n)").bitcast(FP8X4),
@@ -107,19 +156,16 @@ def tile_routed_moe_kernel(tc, xT, w, b, gate, offs, out):
                 in_=laid[:, c:c + n, :, :].rearrange("p c n j -> p (c n j)"),
             )
             for d in range(n):
-                w_codes[(e, g0 + d)] = (codes[:, d, :], scales[:, d, :])
-
-        def multiply(e, g0, n):
-            for g in range(g0, g0 + n):
+                g = g0 + d
                 i, k = PLANES[g]
-                words, c0 = gathered[(("words", g), e)]
-                scales, c1 = gathered[(("scales", i), e)]
+                words, c0 = picked[("words", g, e)]
+                planes, c1 = picked[("scales", i, e)]
                 nc.tensor.matmul_mx(
                     out=sums[e][:],
-                    lhsT=w_codes[(e, g)][0].bitcast(FP8X4),
-                    lhsT_scale=w_codes[(e, g)][1],
+                    lhsT=codes[:, d, :].bitcast(FP8X4),
+                    lhsT_scale=scales[:, d, :],
                     rhs=words[:, c0:c0 + C].bitcast(FP8X4),
-                    rhs_scale=scales[k:P, c1:c1 + C],
+                    rhs_scale=planes[k:P, c1:c1 + C],
                     start=(g == 0),
                     stop=(g == LAST),
                 )
@@ -134,79 +180,34 @@ def tile_routed_moe_kernel(tc, xT, w, b, gate, offs, out):
             squared = tile([P, C], F32, f"squared{e}", buffer)
             nc.scalar.square(squared[:], rectified[e][:])
             nc.vector.tensor_tensor(
-                window[:].indirect(listed(e, e + 1)), squared[:], gates[:, e * C:(e + 1) * C], MULT
+                window[:].indirect(slots(e, e + 1)), squared[:], gates[:, e * C:(e + 1) * C], MULT
             )
 
-        def load(e, g0, n):
-            raw = tile([P, n, J, N], F32, f"w_raw{e}_{g0}")
-            nc.sync.dma_start(raw[:], w_rows[e, :, g0:g0 + n, :, :])
-            for c in range(n):
-                w_raw[(e, g0 + c)] = (raw, c)
-
-        for g in range(PASSES):
-            pieces = []
-            for r0, r1 in X_QUANTS if g in X_PIECES else [(0, T)]:
-                raw = tile([P, 1, J, r1 - r0 + 16], F32, f"x_raw{g}_{r0}")
-                nc.sync.dma_start(raw[:, 0, :, 0:r1 - r0], x_rows[g, :, :, r0:r1])
-                pieces.append((r0, raw))
-            if g == 0:
-                nc.sync.dma_start(offsets[:], offs)
-            if g == 1:
-                nc.sync.dma_start(bias[:], b)
-            laid = tile([P, 1, T, J], BF16, f"laid{g}", f"laid{g % 2}")
-            v = X_VECTOR[g]
-            s = T - X_GPSIMD[g]
-            if s < T:
-                r0, raw = pieces[-1]
-                nc.gpsimd.tensor_copy(laid[:, 0, s:T, :], raw[:, 0, :, s - r0:T - r0].rearrange("p j t -> p t j"))
-            for engine, t0, t1 in [("vector", 0, v), ("scalar", v, 512), ("scalar", 512, s)]:
-                if t1 > t0:
-                    r0, raw = [piece for piece in pieces if piece[0] <= t0][-1]
-                    lay(engine, laid[:, :, t0:t1, :], raw[:, :, :, t0 - r0:t1 - r0])
-            codes = tile([P, T], U32, f"x_words{g}")
-            i, k = PLANES[g]
-            for t0, t1 in X_QUANTS:
-                nc.vector.quantize_mx(
-                    out=codes[:, t0:t1].bitcast(FP8X4),
-                    scales=x_scales[i][k:P, t0:t1],
-                    in_=laid[:, 0, t0:t1, :].rearrange("p t j -> p (t j)"),
-                )
-            x_words.append(codes)
-            if g < LAST:
-                gather_words(g, 0, E)
-            if g == 1:
-                gather_scales(0, 0, E)
-
-        for chunk in W_LOADS:
-            load(*chunk)
-        nc.sync.dma_start(gates[:], gate)
-
-        gather_words(LAST, 0, 1)
-        gather_scales(1, 0, 1)
+        gather("words", LAST, 0, 1)
+        gather("scales", 1, 0, 1)
         group(0, 0, 4)
         cast("scalar", 0, 0, 2)
         cast("scalar", 0, 2, 2)
-        quantise(0, 0, 4)
-        multiply(0, 0, 4)
-        gather_words(LAST, 1, 2, "w_laid0_0")
+        multiply(0, 0, 4, "laid_short")
+        gather("words", LAST, 1, 2, "w_raw0_2")
         group(0, 4, 2)
         cast("scalar", 0, 4, 2)
-        quantise(0, 4, 2)
         multiply(0, 4, 2)
-        gather_scales(1, 1, 2, "w_laid0_4")
-        group(1, 0, 4)
+        gather("scales", 1, 1, 2, "w_raw0_4")
+        group(1, 0, 2)
+        group(1, 2, 2, "w_laid0_4")
         cast("scalar", 1, 0, 2)
+        multiply(1, 0, 2)
         cast("gpsimd", 1, 2, 1)
         cast("scalar", 1, 3, 1)
-        rectify(0, "w_raw1_3")
-        quantise(1, 0, 4)
-        multiply(1, 0, 4)
+        rectify(0, "rectified")
+        multiply(1, 2, 2)
         group(1, 4, 2, "w_raw1_2")
         cast("scalar", 1, 4, 1)
         cast("vector", 1, 5, 1)
-        quantise(1, 4, 2)
-        multiply(1, 4, 2)
-        finish(0, "w_raw1_5")
-        rectify(1)
+        multiply(1, 4, 1)
+        multiply(1, 5, 1)
+        finish(0, "w_laid0_4")
+        rectify(1, "rectified")
         finish(1)
         nc.sync.dma_start(out, window[:])

@@ -24,7 +24,7 @@ PLANES = [(0, 0), (0, 4), (1, 0), (1, 4), (1, 8), (1, 12)]
 LONG = 512
 EARLY_VECTOR = [384, 320]
 LAST_VECTOR = 128
-GPSIMD_TOKENS = 128
+GPSIMD_TOKENS = 160
 W_LOADS = [(0, 0, 2), (0, 2, 2), (0, 4, 2), (1, 0, 2), (1, 2, 1), (1, 3, 1), (1, 4, 1), (1, 5, 1)]
 
 

@@ -24,6 +24,7 @@ PLANES = [(0, 0), (0, 4), (1, 0), (1, 4), (1, 8), (1, 12)]
 LONG = 512
 EARLY_VECTOR = [384, 320]
 LAST_VECTOR = 128
+EDGE = 256
 GPSIMD_TOKENS = 160
 W_LOADS = [(0, 0, 2), (0, 2, 2), (0, 4, 2), (1, 0, 2), (1, 2, 1), (1, 3, 1), (1, 4, 1), (1, 5, 1)]
 
@@ -31,6 +32,7 @@ W_LOADS = [(0, 0, 2), (0, 2, 2), (0, 4, 2), (1, 0, 2), (1, 2, 1), (1, 3, 1), (1,
 def tile_routed_moe_kernel(tc, xT, w, b, gate, offs, out):
     nc = tc.nc
     x_rows = xT.rearrange("(g p j) t -> g p j t", p=P, j=PACK)
+    x_runs = xT.rearrange("(g p j) t -> g p (j t)", p=P, j=PACK)
     w_rows = w.rearrange("e (g p j) n -> e p g j n", p=P, j=PACK)
 
     with ExitStack() as ctx:
@@ -75,16 +77,14 @@ def tile_routed_moe_kernel(tc, xT, w, b, gate, offs, out):
                 picked[(sort, index, e)] = (dense, (e - e0) * C)
 
         for g in range(PASSES):
+            raw = tile([P, 1, PACK, T], F32, f"x_raw{g}")
             if g < LAST:
-                raw = tile([P, 1, PACK, T], F32, f"x_raw{g}")
                 nc.sync.dma_start(raw[:, 0, :, :], x_rows[g])
-                raw_long, raw_short = raw[:, :, :, 0:LONG], raw[:, :, :, LONG:T]
             else:
-                first = tile([P, 1, PACK, LONG], F32, "x_raw_long")
-                nc.sync.dma_start(first[:, 0, :, :], x_rows[g, :, :, 0:LONG])
-                second = tile([P, 1, PACK, T - LONG], F32, "x_raw_short")
-                nc.sync.dma_start(second[:, 0, :, :], x_rows[g, :, :, LONG:T])
-                raw_long, raw_short = first[:], second[:]
+                flat, rows = raw[:].rearrange("p g j t -> p (g j t)"), x_runs[g]
+                for c0, c1 in [(EDGE, PACK * T - EDGE), (0, EDGE), (PACK * T - EDGE, PACK * T)]:
+                    nc.sync.dma_start(flat[:, c0:c1], rows[:, c0:c1])
+            raw_long, raw_short = raw[:, :, :, 0:LONG], raw[:, :, :, LONG:T]
             if g == 0:
                 nc.sync.dma_start(offsets[:], offs)
             laid_long = tile([P, 1, LONG, PACK], BF16, f"laid_long{g}", f"laid_long{g % 2}")
@@ -103,7 +103,11 @@ def tile_routed_moe_kernel(tc, xT, w, b, gate, offs, out):
                     gather("words", g - 1, 0, E)
                 s = T - LONG - GPSIMD_TOKENS
                 interleave("gpsimd", laid_short[:, :, s:T - LONG, :], raw_short[:, :, :, s:T - LONG])
-                interleave("scalar", laid_long[:, :, v:LONG, :], raw_long[:, :, :, v:LONG])
+                if v:
+                    interleave("scalar", laid_long[:, :, EDGE:LONG, :], raw_long[:, :, :, EDGE:LONG])
+                    interleave("scalar", laid_long[:, :, v:EDGE, :], raw_long[:, :, :, v:EDGE])
+                else:
+                    interleave("scalar", laid_long[:], raw_long)
                 interleave("scalar", laid_short[:, :, 0:s, :], raw_short[:, :, :, 0:s])
             words = tile([P, T], U32, f"x_words{g}")
             i, k = PLANES[g]

@@ -99,13 +99,13 @@ def tile_routed_moe_kernel(tc, xT, w, b, gate, offs, out):
             else:
                 v = LAST_VECTOR if g == LAST else 0
                 if v:
-                    interleave("vector", laid_long[:, :, 0:v, :], raw_long[:, :, :, 0:v])
+                    interleave("vector", laid_long[:, :, EDGE:EDGE + v, :], raw_long[:, :, :, EDGE:EDGE + v])
                     gather("words", g - 1, 0, E)
                 s = T - LONG - GPSIMD_TOKENS
                 interleave("gpsimd", laid_short[:, :, s:T - LONG, :], raw_short[:, :, :, s:T - LONG])
                 if v:
-                    interleave("scalar", laid_long[:, :, EDGE:LONG, :], raw_long[:, :, :, EDGE:LONG])
-                    interleave("scalar", laid_long[:, :, v:EDGE, :], raw_long[:, :, :, v:EDGE])
+                    interleave("scalar", laid_long[:, :, EDGE + v:LONG, :], raw_long[:, :, :, EDGE + v:LONG])
+                    interleave("scalar", laid_long[:, :, 0:EDGE, :], raw_long[:, :, :, 0:EDGE])
                 else:
                     interleave("scalar", laid_long[:], raw_long)
                 interleave("scalar", laid_short[:, :, 0:s, :], raw_short[:, :, :, 0:s])

@@ -40,9 +40,9 @@ def tile_routed_moe_kernel(tc, xT, w, b, gate, offs, out):
         psum = ctx.enter_context(tc.psum_pool(name="psum", bufs=1))
 
         def tile(shape, dtype, name, buffer=None):
-            return keep.tile(shape, dtype, name=name, tag=buffer or name, align_bytes=64)
+            return keep.tile(shape, dtype, name=name, tag=buffer or name, align_bytes=256)
 
-        offsets = keep.tile([P, E * C // 16], U16, name="offsets")
+        offsets = keep.tile([P, E * C // 16], U16, name="offsets", align_bytes=256)
         bias = tile([P, E], F32, "bias")
         gates = tile([P, E * C], F32, "gates")
         x_scales = [tile([P, T], U8, f"x_scales{i}") for i in range(2)]

@@ -26,7 +26,9 @@ EARLY_VECTOR = [384, 320]
 LAST_VECTOR = 128
 EDGE = 256
 GPSIMD_TOKENS = 160
-W_LOADS = [(0, 0, 2), (0, 2, 2), (0, 4, 2), (1, 0, 2), (1, 2, 1), (1, 3, 1), (1, 4, 1), (1, 5, 1)]
+SHORT = 4096
+FIRST_RAW = 10240
+W_LOADS = [(0, 0, 2)] + [(0, g, 1) for g in range(2, PASSES)] + [(1, g, 1) for g in range(PASSES)]
 
 
 def tile_routed_moe_kernel(tc, xT, w, b, gate, offs, out):
@@ -37,9 +39,12 @@ def tile_routed_moe_kernel(tc, xT, w, b, gate, offs, out):
 
     with ExitStack() as ctx:
         keep = ctx.enter_context(tc.tile_pool(name="keep", bufs=1))
+        shared = ctx.enter_context(tc.tile_pool(name="shared", bufs=1))
         psum = ctx.enter_context(tc.psum_pool(name="psum", bufs=1))
 
         def tile(shape, dtype, name, buffer=None):
+            if isinstance(buffer, int):
+                return shared.tile(shape, dtype, name=name, align_bytes=256, offset=buffer)
             return keep.tile(shape, dtype, name=name, tag=buffer or name, align_bytes=256)
 
         offsets = keep.tile([P, E * C // 16], U16, name="offsets", align_bytes=256)
@@ -88,7 +93,9 @@ def tile_routed_moe_kernel(tc, xT, w, b, gate, offs, out):
             if g == 0:
                 nc.sync.dma_start(offsets[:], offs)
             laid_long = tile([P, 1, LONG, PACK], BF16, f"laid_long{g}", f"laid_long{g % 2}")
-            laid_short = tile([P, 1, T - LONG, PACK], BF16, f"laid_short{g}", "laid_short")
+            laid_short = shared.tile(
+                [P, 1, T - LONG, PACK], BF16, name=f"laid_short{g}", tag="laid_short", align_bytes=256, offset=SHORT
+            )
             parts = [(0, LONG, laid_long), (LONG, T, laid_short)]
             if g < len(EARLY_VECTOR):
                 v = EARLY_VECTOR[g]
@@ -125,7 +132,7 @@ def tile_routed_moe_kernel(tc, xT, w, b, gate, offs, out):
 
         w_raw = {}
         for e, g0, n in W_LOADS:
-            raw = tile([P, n, PACK, N], F32, f"w_raw{e}_{g0}")
+            raw = tile([P, n, PACK, N], F32, f"w_raw{e}_{g0}", FIRST_RAW if (e, g0) == (0, 0) else None)
             nc.sync.dma_start(raw[:], w_rows[e, :, g0:g0 + n, :, :])
             for c in range(n):
                 w_raw[(e, g0 + c)] = (raw, c)
@@ -135,32 +142,34 @@ def tile_routed_moe_kernel(tc, xT, w, b, gate, offs, out):
 
         w_laid = {}
 
-        def group(e, g0, n, buffer=None):
-            laid = tile([P, n, N, PACK], BF16, f"w_laid{e}_{g0}", buffer)
-            for c in range(n):
-                w_laid[(e, g0 + c)] = (laid, c)
+        def group(e, passes, buffer=None):
+            laid = tile([P, len(passes), N, PACK], BF16, f"w_laid{e}_{passes[0]}", buffer)
+            for c, g in enumerate(passes):
+                w_laid[(e, g)] = (laid, c)
 
-        def cast(engine, e, g0, n):
-            raw, r = w_raw[(e, g0)]
-            laid, c = w_laid[(e, g0)]
+        def cast(engine, e, g):
+            raw, r = w_raw[(e, g)]
+            laid, c = w_laid[(e, g)]
             if engine == "gpsimd":
                 nc.gpsimd.tensor_scalar(
                     laid[:, c, :, :], raw[:, r, :, :].rearrange("p j t -> p t j"), 1.0, 0.0, MULT, ADD
                 )
             else:
-                interleave(engine, laid[:, c:c + n, :, :], raw[:, r:r + n, :, :])
+                interleave(engine, laid[:, c:c + 1, :, :], raw[:, r:r + 1, :, :])
 
-        def multiply(e, g0, n, buffer=None):
-            laid, c = w_laid[(e, g0)]
-            codes = tile([P, n, N], U32, f"w_words{e}_{g0}", buffer)
-            scales = tile([P, n, N], U8, f"w_scales{e}_{g0}")
+        multiplied = [0] * E
+
+        def multiply(e, passes, buffer=None):
+            n = len(passes)
+            laid, c = w_laid[(e, passes[0])]
+            codes = tile([P, n, N], U32, f"w_words{e}_{passes[0]}")
+            scales = tile([P, n, N], U8, f"w_scales{e}_{passes[0]}", buffer)
             nc.vector.quantize_mx(
                 out=codes[:].rearrange("p c n -> p (c n)").bitcast(FP8X4),
                 scales=scales[:].rearrange("p c n -> p (c n)"),
                 in_=laid[:, c:c + n, :, :].rearrange("p c n j -> p (c n j)"),
             )
-            for d in range(n):
-                g = g0 + d
+            for d, g in enumerate(passes):
                 i, k = PLANES[g]
                 words, c0 = picked[("words", g, e)]
                 planes, c1 = picked[("scales", i, e)]
@@ -170,9 +179,10 @@ def tile_routed_moe_kernel(tc, xT, w, b, gate, offs, out):
                     lhsT_scale=scales[:, d, :],
                     rhs=words[:, c0:c0 + C].bitcast(FP8X4),
                     rhs_scale=planes[k:P, c1:c1 + C],
-                    start=(g == 0),
-                    stop=(g == LAST),
+                    start=(multiplied[e] == 0),
+                    stop=(multiplied[e] == LAST),
                 )
+                multiplied[e] += 1
 
         rectified = {}
 
@@ -189,29 +199,31 @@ def tile_routed_moe_kernel(tc, xT, w, b, gate, offs, out):
 
         gather("words", LAST, 0, 1)
         gather("scales", 1, 0, 1)
-        group(0, 0, 4)
-        cast("scalar", 0, 0, 2)
-        cast("scalar", 0, 2, 2)
-        multiply(0, 0, 4, "laid_short")
-        gather("words", LAST, 1, 2, "w_raw0_2")
-        group(0, 4, 2)
-        cast("scalar", 0, 4, 2)
-        multiply(0, 4, 2)
-        gather("scales", 1, 1, 2, "w_raw0_4")
-        group(1, 0, 2)
-        group(1, 2, 2, "w_laid0_4")
-        cast("scalar", 1, 0, 2)
-        multiply(1, 0, 2)
-        cast("gpsimd", 1, 2, 1)
-        cast("scalar", 1, 3, 1)
+        group(0, [1, 2, 3])
+        group(0, [4, 5, 0], SHORT + 256 - 3072)
+        cast("gpsimd", 0, 0)
+        for g in [1, 2, 3]:
+            cast("scalar", 0, g)
+        multiply(0, [1, 2, 3], SHORT + 256)
+        gather("words", LAST, 1, 2, "w_raw0_3")
+        for g in [4, 5]:
+            cast("scalar", 0, g)
+        multiply(0, [4, 5, 0])
+        gather("scales", 1, 1, 2, FIRST_RAW)
+        group(1, [0, 1, 2, 3], SHORT + 2048 - 256)
+        for g in [0, 1]:
+            cast("scalar", 1, g)
+        multiply(1, [0, 1], FIRST_RAW + 256)
+        for g in [2, 3]:
+            cast("scalar", 1, g)
         rectify(0, "rectified")
-        multiply(1, 2, 2)
-        group(1, 4, 2, "w_raw1_2")
-        cast("scalar", 1, 4, 1)
-        cast("vector", 1, 5, 1)
-        multiply(1, 4, 1)
-        multiply(1, 5, 1)
-        finish(0, "w_laid0_4")
+        multiply(1, [2, 3], FIRST_RAW + 512)
+        group(1, [4, 5], FIRST_RAW + 1024)
+        cast("scalar", 1, 4)
+        cast("vector", 1, 5)
+        multiply(1, [4])
+        multiply(1, [5])
+        finish(0, "w_raw1_4")
         rectify(1, "rectified")
         finish(1)
         nc.sync.dma_start(out, window[:])

@@ -13,6 +13,7 @@ U8 = mybir.dt.uint8
 FP8X4 = mybir.dt.float8_e4m3fn_x4
 MULT = mybir.AluOpType.mult
 ADD = mybir.AluOpType.add
+MAX = mybir.AluOpType.max
 RELU = mybir.ActivationFunctionType.Relu
 
 P = 128
@@ -28,6 +29,7 @@ EDGE = 256
 GPSIMD_TOKENS = 160
 SHORT = 4096
 FIRST_RAW = 10240
+LAST_CODES = 16384
 W_LOADS = [(0, 0, 2)] + [(0, g, 1) for g in range(2, PASSES)] + [(1, g, 1) for g in range(PASSES)]
 
 
@@ -136,9 +138,10 @@ def tile_routed_moe_kernel(tc, xT, w, b, gate, offs, out):
             nc.sync.dma_start(raw[:], w_rows[e, :, g0:g0 + n, :, :])
             for c in range(n):
                 w_raw[(e, g0 + c)] = (raw, c)
-            if (e, g0) == (1, 3):
+            if (e, g0) == (1, 2):
                 nc.sync.dma_start(bias[:], b)
-        nc.sync.dma_start(gates[:], gate)
+        for e in range(E):
+            nc.sync.dma_start(gates[:, e * C:(e + 1) * C], gate[:, e * C:(e + 1) * C])
 
         w_laid = {}
 
@@ -147,7 +150,7 @@ def tile_routed_moe_kernel(tc, xT, w, b, gate, offs, out):
             for c, g in enumerate(passes):
                 w_laid[(e, g)] = (laid, c)
 
-        def cast(engine, e, g):
+        def cast(engine, e, g, n0=0, n1=N):
             raw, r = w_raw[(e, g)]
             laid, c = w_laid[(e, g)]
             if engine == "gpsimd":
@@ -155,14 +158,14 @@ def tile_routed_moe_kernel(tc, xT, w, b, gate, offs, out):
                     laid[:, c, :, :], raw[:, r, :, :].rearrange("p j t -> p t j"), 1.0, 0.0, MULT, ADD
                 )
             else:
-                interleave(engine, laid[:, c:c + 1, :, :], raw[:, r:r + 1, :, :])
+                interleave(engine, laid[:, c:c + 1, n0:n1, :], raw[:, r:r + 1, :, n0:n1])
 
         multiplied = [0] * E
 
-        def multiply(e, passes, buffer=None):
+        def multiply(e, passes, buffer=None, codes_buffer=None):
             n = len(passes)
             laid, c = w_laid[(e, passes[0])]
-            codes = tile([P, n, N], U32, f"w_words{e}_{passes[0]}")
+            codes = tile([P, n, N], U32, f"w_words{e}_{passes[0]}", codes_buffer)
             scales = tile([P, n, N], U8, f"w_scales{e}_{passes[0]}", buffer)
             nc.vector.quantize_mx(
                 out=codes[:].rearrange("p c n -> p (c n)").bitcast(FP8X4),
@@ -186,9 +189,12 @@ def tile_routed_moe_kernel(tc, xT, w, b, gate, offs, out):
 
         rectified = {}
 
-        def rectify(e, buffer=None):
-            rectified[e] = tile([P, C], F32, f"rectified{e}", buffer)
-            nc.scalar.activation(rectified[e][:], sums[e][:], RELU, bias=bias[:, e:e + 1])
+        def rectify(engine, e):
+            rectified[e] = tile([P, C], F32, f"rectified{e}")
+            if engine == "scalar":
+                nc.scalar.activation(rectified[e][:], sums[e][:], RELU, bias=bias[:, e:e + 1])
+            else:
+                nc.vector.tensor_scalar(rectified[e][:], sums[e][:], bias[:, e:e + 1], 0.0, ADD, MAX)
 
         def finish(e, buffer=None):
             squared = tile([P, C], F32, f"squared{e}", buffer)
@@ -205,25 +211,26 @@ def tile_routed_moe_kernel(tc, xT, w, b, gate, offs, out):
         for g in [1, 2, 3]:
             cast("scalar", 0, g)
         multiply(0, [1, 2, 3], SHORT + 256)
-        gather("words", LAST, 1, 2, "w_raw0_3")
         for g in [4, 5]:
             cast("scalar", 0, g)
-        multiply(0, [4, 5, 0])
+        multiply(0, [4, 5, 0], None, LAST_CODES)
+        gather("words", LAST, 1, 2, FIRST_RAW + 3072)
         gather("scales", 1, 1, 2, FIRST_RAW)
         group(1, [0, 1, 2, 3], SHORT + 2048 - 256)
         for g in [0, 1]:
             cast("scalar", 1, g)
         multiply(1, [0, 1], FIRST_RAW + 256)
+        rectify("vector", 0)
         for g in [2, 3]:
             cast("scalar", 1, g)
-        rectify(0, "rectified")
-        multiply(1, [2, 3], FIRST_RAW + 512)
-        group(1, [4, 5], FIRST_RAW + 1024)
+        multiply(1, [2, 3], LAST_CODES)
+        group(1, [4, 5], LAST_CODES + 256)
         cast("scalar", 1, 4)
-        cast("vector", 1, 5)
+        cast("scalar", 1, 5, 0, N // 2)
+        cast("vector", 1, 5, N // 2, N)
         multiply(1, [4])
         multiply(1, [5])
-        finish(0, "w_raw1_4")
-        rectify(1, "rectified")
+        finish(0)
+        rectify("scalar", 1)
         finish(1)
         nc.sync.dma_start(out, window[:])

@@ -30,7 +30,9 @@ GPSIMD_TOKENS = 160
 SHORT = 4096
 FIRST_RAW = 10240
 LAST_CODES = 16384
-W_LOADS = [(0, 0, 2)] + [(0, g, 1) for g in range(2, PASSES)] + [(1, g, 1) for g in range(PASSES)]
+LAST_RAW = 20480
+PASS0_RAW = 32768
+W_LOADS = [(0, 0, 1), (0, 1, 2)] + [(0, g, 1) for g in range(3, PASSES)] + [(1, g, 1) for g in range(PASSES)]
 
 
 def tile_routed_moe_kernel(tc, xT, w, b, gate, offs, out):
@@ -84,7 +86,7 @@ def tile_routed_moe_kernel(tc, xT, w, b, gate, offs, out):
                 picked[(sort, index, e)] = (dense, (e - e0) * C)
 
         for g in range(PASSES):
-            raw = tile([P, 1, PACK, T], F32, f"x_raw{g}")
+            raw = tile([P, 1, PACK, T], F32, f"x_raw{g}", LAST_RAW if g == LAST else None)
             if g < LAST:
                 nc.sync.dma_start(raw[:, 0, :, :], x_rows[g])
             else:
@@ -134,7 +136,7 @@ def tile_routed_moe_kernel(tc, xT, w, b, gate, offs, out):
 
         w_raw = {}
         for e, g0, n in W_LOADS:
-            raw = tile([P, n, PACK, N], F32, f"w_raw{e}_{g0}", FIRST_RAW if (e, g0) == (0, 0) else None)
+            raw = tile([P, n, PACK, N], F32, f"w_raw{e}_{g0}", {(0, 0): PASS0_RAW, (0, 1): FIRST_RAW}.get((e, g0)))
             nc.sync.dma_start(raw[:], w_rows[e, :, g0:g0 + n, :, :])
             for c in range(n):
                 w_raw[(e, g0 + c)] = (raw, c)
@@ -162,7 +164,7 @@ def tile_routed_moe_kernel(tc, xT, w, b, gate, offs, out):
 
         multiplied = [0] * E
 
-        def multiply(e, passes, buffer=None, codes_buffer=None):
+        def quantise(e, passes, buffer=None, codes_buffer=None):
             n = len(passes)
             laid, c = w_laid[(e, passes[0])]
             codes = tile([P, n, N], U32, f"w_words{e}_{passes[0]}", codes_buffer)
@@ -172,6 +174,9 @@ def tile_routed_moe_kernel(tc, xT, w, b, gate, offs, out):
                 scales=scales[:].rearrange("p c n -> p (c n)"),
                 in_=laid[:, c:c + n, :, :].rearrange("p c n j -> p (c n j)"),
             )
+            return e, passes, codes, scales
+
+        def accumulate(e, passes, codes, scales):
             for d, g in enumerate(passes):
                 i, k = PLANES[g]
                 words, c0 = picked[("words", g, e)]
@@ -186,6 +191,9 @@ def tile_routed_moe_kernel(tc, xT, w, b, gate, offs, out):
                     stop=(multiplied[e] == LAST),
                 )
                 multiplied[e] += 1
+
+        def multiply(e, passes, buffer=None, codes_buffer=None):
+            accumulate(*quantise(e, passes, buffer, codes_buffer))
 
         rectified = {}
 
@@ -203,23 +211,26 @@ def tile_routed_moe_kernel(tc, xT, w, b, gate, offs, out):
                 window[:].indirect(slots(e, e + 1)), squared[:], gates[:, e * C:(e + 1) * C], MULT
             )
 
-        gather("words", LAST, 0, 1)
-        gather("scales", 1, 0, 1)
-        group(0, [1, 2, 3])
-        group(0, [4, 5, 0], SHORT + 256 - 3072)
-        cast("gpsimd", 0, 0)
-        for g in [1, 2, 3]:
+        group(0, [0])
+        cast("scalar", 0, 0)
+        first = quantise(0, [0], LAST_RAW)
+        gather("scales", 1, 0, 1, PASS0_RAW)
+        gather("words", LAST, 0, 1, PASS0_RAW + 256)
+        accumulate(*first)
+        group(0, [2, 3, 4])
+        group(0, [5, 1], SHORT + 256 - 2048)
+        cast("gpsimd", 0, 1)
+        for g in [2, 3, 4]:
             cast("scalar", 0, g)
-        multiply(0, [1, 2, 3], SHORT + 256)
-        for g in [4, 5]:
-            cast("scalar", 0, g)
-        multiply(0, [4, 5, 0], None, LAST_CODES)
+        multiply(0, [2, 3, 4], SHORT + 256)
+        cast("scalar", 0, 5)
+        multiply(0, [5, 1], None, LAST_CODES)
         gather("words", LAST, 1, 2, FIRST_RAW + 3072)
-        gather("scales", 1, 1, 2, FIRST_RAW)
+        gather("scales", 1, 1, 2, FIRST_RAW + 2048)
         group(1, [0, 1, 2, 3], SHORT + 2048 - 256)
         for g in [0, 1]:
             cast("scalar", 1, g)
-        multiply(1, [0, 1], FIRST_RAW + 256)
+        multiply(1, [0, 1], FIRST_RAW + 2048 + 256)
         rectify("vector", 0)
         for g in [2, 3]:
             cast("scalar", 1, g)

from contextlib import ExitStack

import concourse.mybir as mybir

K, T, E, C, N = 3072, 768, 2, 256, 128
FLOPS = 2 * K * N * E * C

F32 = mybir.dt.float32
BF16 = mybir.dt.bfloat16
U32 = mybir.dt.uint32
U16 = mybir.dt.uint16
U8 = mybir.dt.uint8
FP8X4 = mybir.dt.float8_e4m3fn_x4
MULT = mybir.AluOpType.mult
ADD = mybir.AluOpType.add
MAX = mybir.AluOpType.max
RELU = mybir.ActivationFunctionType.Relu

P = 128
PACK = 4
PAIR = 2
PASSES = K // (P * PACK)
LAST = PASSES - 1
PLANES = [(0, 0), (0, 4), (1, 0), (1, 4), (1, 8), (1, 12)]
LONG = 512
EARLY_VECTOR = [384, 320]
LAST_VECTOR = 128
EDGE = 256
GPSIMD_TOKENS = 160
SHORT = 4096
FIRST_RAW = 10240
LAST_CODES = 16384
LAST_RAW = 20480
PASS0_RAW = 32768
W_LOADS = [(0, 0, 1), (0, 1, 2)] + [(0, g, 1) for g in range(3, PASSES)] + [(1, g, 1) for g in range(PASSES)]


def tile_routed_moe_kernel(tc, xT, w, b, gate, offs, out):
    nc = tc.nc
    x_rows = xT.rearrange("(g p j) t -> g p j t", p=P, j=PACK)
    x_runs = xT.rearrange("(g p j) t -> g p (j t)", p=P, j=PACK)
    w_rows = w.rearrange("e (g p j) n -> e p g j n", p=P, j=PACK)

    with ExitStack() as ctx:
        keep = ctx.enter_context(tc.tile_pool(name="keep", bufs=1))
        shared = ctx.enter_context(tc.tile_pool(name="shared", bufs=1))
        psum = ctx.enter_context(tc.psum_pool(name="psum", bufs=1))

        def tile(shape, dtype, name, buffer=None):
            if isinstance(buffer, int):
                return shared.tile(shape, dtype, name=name, align_bytes=256, offset=buffer)
            return keep.tile(shape, dtype, name=name, tag=buffer or name, align_bytes=256)

        offsets = keep.tile([P, E * C // 16], U16, name="offsets", align_bytes=256)
        bias = tile([P, E], F32, "bias")
        gates = tile([P, E * C], F32, "gates")
        x_scales = [tile([P, T], U8, f"x_scales{i}") for i in range(2)]
        for plane in x_scales:
            nc.gpsimd.memset(plane[:], 0)
        window = tile([P, T], F32, "window")
        nc.gpsimd.memset(window[:], 0.0)
        sums = [psum.tile([P, C], F32, name=f"sums{e}") for e in range(E)]

        def slots(e0, e1):
            return offsets[:, e0 * C // 16:e1 * C // 16]

        def interleave(engine, laid, raw):
            if engine == "gpsimd":
                nc.gpsimd.tensor_copy(laid[:, 0, :, :], raw[:, 0, :, :].rearrange("p j t -> p t j"))
                return
            laid = laid.rearrange("p g (c i) j -> p g c j i", i=PAIR)
            raw = raw.rearrange("p g j (c i) -> p g c j i", i=PAIR)
            if engine == "scalar":
                nc.scalar.copy(laid, raw)
            else:
                nc.vector.tensor_copy(laid, raw)

        x_words = []
        picked = {}

        def gather(sort, index, e0, e1, buffer=None):
            source, dtype = (x_words[index], U32) if sort == "words" else (x_scales[index], U8)
            dense = tile([P, (e1 - e0) * C], dtype, f"picked_{sort}{index}_{e0}", buffer)
            nc.vector.tensor_copy(dense[:], source[:].indirect(slots(e0, e1)))
            for e in range(e0, e1):
                picked[(sort, index, e)] = (dense, (e - e0) * C)

        for g in range(PASSES):
            raw = tile([P, 1, PACK, T], F32, f"x_raw{g}", LAST_RAW if g == LAST else None)
            if g < LAST:
                nc.sync.dma_start(raw[:, 0, :, :], x_rows[g])
            else:
                flat, rows = raw[:].rearrange("p g j t -> p (g j t)"), x_runs[g]
                for c0, c1 in [(EDGE, PACK * T - EDGE), (0, EDGE), (PACK * T - EDGE, PACK * T)]:
                    nc.sync.dma_start(flat[:, c0:c1], rows[:, c0:c1])
            raw_long, raw_short = raw[:, :, :, 0:LONG], raw[:, :, :, LONG:T]
            if g == 0:
                nc.sync.dma_start(offsets[:], offs)
            laid_long = tile([P, 1, LONG, PACK], BF16, f"laid_long{g}", f"laid_long{g % 2}")
            laid_short = shared.tile(
                [P, 1, T - LONG, PACK], BF16, name=f"laid_short{g}", tag="laid_short", align_bytes=256, offset=SHORT
            )
            parts = [(0, LONG, laid_long), (LONG, T, laid_short)]
            if g < len(EARLY_VECTOR):
                v = EARLY_VECTOR[g]
                interleave("vector", laid_long[:, :, 0:v, :], raw_long[:, :, :, 0:v])
                interleave("scalar", laid_short[:], raw_short)
                interleave("scalar", laid_long[:, :, v:LONG, :], raw_long[:, :, :, v:LONG])
                parts = parts[::-1]
            else:
                v = LAST_VECTOR if g == LAST else 0
                if v:
                    interleave("vector", laid_long[:, :, EDGE:EDGE + v, :], raw_long[:, :, :, EDGE:EDGE + v])
                    gather("words", g - 1, 0, E)
                s = T - LONG - GPSIMD_TOKENS
                interleave("gpsimd", laid_short[:, :, s:T - LONG, :], raw_short[:, :, :, s:T - LONG])
                if v:
                    interleave("scalar", laid_long[:, :, EDGE + v:LONG, :], raw_long[:, :, :, EDGE + v:LONG])
                    interleave("scalar", laid_long[:, :, 0:EDGE, :], raw_long[:, :, :, 0:EDGE])
                else:
                    interleave("scalar", laid_long[:], raw_long)
                interleave("scalar", laid_short[:, :, 0:s, :], raw_short[:, :, :, 0:s])
            words = tile([P, T], U32, f"x_words{g}")
            i, k = PLANES[g]
            for t0, t1, laid in parts:
                nc.vector.quantize_mx(
                    out=words[:, t0:t1].bitcast(FP8X4),
                    scales=x_scales[i][k:P, t0:t1],
                    in_=laid[:].rearrange("p g t j -> p (g t j)"),
                )
            x_words.append(words)
            if g < LAST - 1:
                gather("words", g, 0, E)
            if g == 1:
                gather("scales", 0, 0, E)

        w_raw = {}
        for e, g0, n in W_LOADS:
            raw = tile([P, n, PACK, N], F32, f"w_raw{e}_{g0}", {(0, 0): PASS0_RAW, (0, 1): FIRST_RAW}.get((e, g0)))
            nc.sync.dma_start(raw[:], w_rows[e, :, g0:g0 + n, :, :])
            for c in range(n):
                w_raw[(e, g0 + c)] = (raw, c)
            if (e, g0) == (1, 2):
                nc.sync.dma_start(bias[:], b)
        for e in range(E):
            nc.sync.dma_start(gates[:, e * C:(e + 1) * C], gate[:, e * C:(e + 1) * C])

        w_laid = {}

        def group(e, passes, buffer=None):
            laid = tile([P, len(passes), N, PACK], BF16, f"w_laid{e}_{passes[0]}", buffer)
            for c, g in enumerate(passes):
                w_laid[(e, g)] = (laid, c)

        def cast(engine, e, g, n0=0, n1=N):
            raw, r = w_raw[(e, g)]
            laid, c = w_laid[(e, g)]
            if engine == "gpsimd":
                nc.gpsimd.tensor_scalar(
                    laid[:, c, :, :], raw[:, r, :, :].rearrange("p j t -> p t j"), 1.0, 0.0, MULT, ADD
                )
            else:
                interleave(engine, laid[:, c:c + 1, n0:n1, :], raw[:, r:r + 1, :, n0:n1])

        multiplied = [0] * E

        def quantise(e, passes, buffer=None, codes_buffer=None):
            n = len(passes)
            laid, c = w_laid[(e, passes[0])]
            codes = tile([P, n, N], U32, f"w_words{e}_{passes[0]}", codes_buffer)
            scales = tile([P, n, N], U8, f"w_scales{e}_{passes[0]}", buffer)
            nc.vector.quantize_mx(
                out=codes[:].rearrange("p c n -> p (c n)").bitcast(FP8X4),
                scales=scales[:].rearrange("p c n -> p (c n)"),
                in_=laid[:, c:c + n, :, :].rearrange("p c n j -> p (c n j)"),
            )
            return e, passes, codes, scales

        def accumulate(e, passes, codes, scales):
            for d, g in enumerate(passes):
                i, k = PLANES[g]
                words, c0 = picked[("words", g, e)]
                planes, c1 = picked[("scales", i, e)]
                nc.tensor.matmul_mx(
                    out=sums[e][:],
                    lhsT=codes[:, d, :].bitcast(FP8X4),
                    lhsT_scale=scales[:, d, :],
                    rhs=words[:, c0:c0 + C].bitcast(FP8X4),
                    rhs_scale=planes[k:P, c1:c1 + C],
                    start=(multiplied[e] == 0),
                    stop=(multiplied[e] == LAST),
                )
                multiplied[e] += 1

        def multiply(e, passes, buffer=None, codes_buffer=None):
            accumulate(*quantise(e, passes, buffer, codes_buffer))

        rectified = {}

        def rectify(engine, e):
            rectified[e] = tile([P, C], F32, f"rectified{e}")
            if engine == "scalar":
                nc.scalar.activation(rectified[e][:], sums[e][:], RELU, bias=bias[:, e:e + 1])
            else:
                nc.vector.tensor_scalar(rectified[e][:], sums[e][:], bias[:, e:e + 1], 0.0, ADD, MAX)

        def finish(e, buffer=None):
            squared = tile([P, C], F32, f"squared{e}", buffer)
            nc.scalar.square(squared[:], rectified[e][:])
            nc.vector.tensor_tensor(
                window[:].indirect(slots(e, e + 1)), squared[:], gates[:, e * C:(e + 1) * C], MULT
            )

        group(0, [0])
        cast("scalar", 0, 0)
        first = quantise(0, [0], LAST_RAW)
        gather("scales", 1, 0, 1, PASS0_RAW)
        gather("words", LAST, 0, 1, PASS0_RAW + 256)
        accumulate(*first)
        group(0, [2, 3, 4])
        group(0, [5, 1], SHORT + 256 - 2048)
        cast("gpsimd", 0, 1)
        for g in [2, 3, 4]:
            cast("scalar", 0, g)
        multiply(0, [2, 3, 4], SHORT + 256)
        cast("scalar", 0, 5)
        multiply(0, [5, 1], None, LAST_CODES)
        gather("words", LAST, 1, 2, FIRST_RAW + 3072)
        gather("scales", 1, 1, 2, FIRST_RAW + 2048)
        group(1, [0, 1, 2, 3], SHORT + 2048 - 256)
        for g in [0, 1]:
            cast("scalar", 1, g)
        multiply(1, [0, 1], FIRST_RAW + 2048 + 256)
        rectify("vector", 0)
        for g in [2, 3]:
            cast("scalar", 1, g)
        multiply(1, [2, 3], LAST_CODES)
        group(1, [4, 5], LAST_CODES + 256)
        cast("scalar", 1, 4)
        cast("scalar", 1, 5, 0, N // 2)
        cast("vector", 1, 5, N // 2, N)
        multiply(1, [4])
        multiply(1, [5])
        finish(0)
        rectify("scalar", 1)
        finish(1)
        nc.sync.dma_start(out, window[:])
